import numpy as np
import ml_dtypes


def mxq(x, axis, fmt="e4m3"):
    dtype, down = {"e4m3": (ml_dtypes.float8_e4m3fn, 7), "e5m2": (ml_dtypes.float8_e5m2, 14)}[fmt]
    v = np.moveaxis(np.asarray(x, np.float32).astype(ml_dtypes.bfloat16).astype(np.float64), axis, -1)
    blocks = v.reshape(v.shape[:-1] + (-1, 32))
    amax = np.abs(blocks).max(-1, keepdims=True)
    byte = np.maximum(np.where(amax > 0, np.frexp(amax)[1] - 1 + 127, 0) - down, 1)
    scale = np.exp2(byte - 127.0)
    codes = (blocks / scale).astype(np.float32).astype(dtype).astype(np.float64)
    return np.moveaxis((codes * scale).reshape(v.shape), -1, axis)


WIDE = False


def mx_kscale(k):
    if not WIDE:
        return np.ones(k)
    levels = np.array([10, -10, 5, -5, 0])
    if k % 512:
        return np.exp2(np.random.permutation(np.resize(levels, k // 32))).repeat(32)
    a = np.empty((k // 512, 16))
    for p in range(k // 512):
        a[p, :8] = np.random.permutation(np.resize(levels, 8))
        for g in range(8):
            far = levels[np.abs(levels - a[p, g]) >= 10]
            a[p, g + 8] = far[np.random.randint(len(far))]
    return np.exp2(a.ravel()).repeat(32)


BF16 = ml_dtypes.bfloat16


def bf(x):
    return np.asarray(x, np.float32).astype(BF16)


def f64(x):
    return np.asarray(x).astype(np.float64)


E2M1 = np.array([0.0, 0.5, 1.0, 1.5, 2.0, 3.0, 4.0, 6.0, -0.0, -0.5, -1.0, -1.5, -2.0, -3.0, -4.0, -6.0])


def pack_weight(w, fmt):
    k, n = w.shape
    w = f64(bf(w)).reshape(k // 32, 32, n)
    amax = np.abs(w).max(1)
    if fmt == "e4m3":
        byte = np.frexp(amax)[1] - 1 + 127 - 7
    else:
        mant, ex = np.frexp(amax / 6.0)
        byte = np.where(mant > 0.5, ex, ex - 1) + 127
    byte = np.clip(np.where(amax > 0, byte, 1), 1, 254)
    scaled = (w * np.exp2(127.0 - byte)[:, None, :]).reshape(k, n).astype(np.float32)
    by_word = np.ascontiguousarray(scaled.reshape(k // 512, 128, 4, n).transpose(0, 1, 3, 2))
    if fmt == "e4m3":
        words = by_word.astype(ml_dtypes.float8_e4m3fn).view(np.uint8)
    else:
        c = by_word.astype(ml_dtypes.float4_e2m1fn).view(np.uint8) & 0xF
        words = c[..., 0::2] | (c[..., 1::2] << 4)
    return np.ascontiguousarray(words), np.ascontiguousarray(byte.astype(np.uint8).reshape(k // 512, 16, n))


def unpack_weight(words, scales, fmt):
    g, p, n, _ = words.shape
    if fmt == "e4m3":
        vals = np.ascontiguousarray(words).view(ml_dtypes.float8_e4m3fn).astype(np.float64)
    else:
        nib = np.empty((g, p, n, 4), np.uint8)
        nib[..., 0::2] = words & 0xF
        nib[..., 1::2] = words >> 4
        vals = E2M1[nib]
    vals = vals * np.repeat(np.exp2(scales.astype(np.float64) - 127.0), 8, axis=1)[..., None]
    return vals.transpose(0, 1, 3, 2).reshape(g * 512, n)
def pack4(w):
    words, scales = pack_weight(w, "e2m1")
    return words.reshape(words.shape[0], 128, -1), scales


def unpack4(words, scales):
    return unpack_weight(words.reshape(words.shape[0], 128, -1, 2), scales, "e2m1")


def planes(Y):
    n, m = Y.shape
    b = f64(bf(Y)).reshape(n // 32, 32, m)
    amax = np.abs(b).max(1)
    byte = np.clip(np.where(amax > 0, np.frexp(amax)[1] - 1 + 127 - 7, 1), 1, 254)
    codes = (b * np.exp2(127.0 - byte)[:, None, :]).reshape(n, m).astype(np.float32).astype(ml_dtypes.float8_e4m3fn).view(np.uint8)
    words = codes.reshape(n // 512, 128, 4, m).transpose(0, 1, 3, 2)
    return np.ascontiguousarray(words), np.ascontiguousarray(byte.astype(np.uint8).reshape(n // 512, 16, m))


S, R, G, N = 768, 1024, 2048, 1536

def setup_inputs():
    s = mx_kscale(R)
    t = mx_kscale(G)
    x = np.random.randn(S, R) * s[None, :]
    w = 2.0 * np.random.randn(R, G) / np.sqrt(R) / s[:, None]
    w_words, w_scales = pack4(w)
    rate = np.exp(0.3 * np.random.randn(G)) * t
    spread = np.exp(0.8 * np.random.randn(N))
    tr = 1.5 * np.random.randn(G, N) / np.sqrt(G) * spread[None, :] / t[:, None]
    t_words, t_scales = pack4(tr)
    decay = np.exp(0.3 * np.random.randn(N))
    level = np.exp(0.3 * np.random.randn(S, N)) * spread[None, :]
    return {"x": bf(x), "w_words": w_words, "w_scales": w_scales, "rate": bf(rate),
            "t_words": t_words, "t_scales": t_scales, "decay": bf(decay), "level": bf(level)}

def reference(x, w_words, w_scales, rate, t_words, t_scales, decay, level):
    xq = mxq(f64(x), 1, "e4m3")
    w = unpack4(w_words, w_scales)
    tr = unpack4(t_words, t_scales)
    z = xq @ w
    h = f64(rate)[None, :] / (1.0 + np.exp(-z))
    hq = mxq(h, 1, "e4m3")
    y = (hq @ tr) - f64(decay)[None, :] * f64(level)
    Y = y.T
    words, scales = planes(Y)
    return y, words, scales

@@ -1,0 +1,352 @@
+from contextlib import ExitStack
+
+import concourse.mybir as mybir
+from concourse.masks import make_identity
+
+S, R, G, N = 768, 1024, 2048, 1536
+FLOPS = 2 * S * R * G + 2 * S * G * N
+
+F32 = mybir.dt.float32
+BF16 = mybir.dt.bfloat16
+I32 = mybir.dt.int32
+U32 = mybir.dt.uint32
+U8 = mybir.dt.uint8
+FP8X4 = mybir.dt.float8_e4m3fn_x4
+FP4X4 = mybir.dt.float4_e2m1fn_x4
+ACT = mybir.ActivationFunctionType
+ALU = mybir.AluOpType
+
+P = 128
+KP = 512
+TILES = S // P
+RG, GG, NG = R // KP, G // KP, N // KP
+BANKS = 8
+
+
+def schedule():
+    order = []
+
+    def put(name, i, *ks):
+        if 0 <= i < TILES:
+            order.extend((name, i, k) for k in (ks or (0,)))
+
+    last = TILES - 1
+    put("t_x", 0)
+    put("t_rate", 0, 0, 1)
+    put("c_x", 0)
+    put("q_x", 0)
+    put("c_rate", 0, 0, 1)
+    for j in range(TILES + 2):
+        a, b = j, j - 2
+        put("mm1", a, 0)
+        if j > 0:
+            put("c_x", j + 1)
+            put("q_x", j + 1)
+        put("c_y", j - 4, 0)
+        put("dl", j - 1, 0)
+        put("sig", a, 0)
+        put("mm1", a, 1)
+        if j == 0:
+            put("t_x", 1)
+            put("t_decay", 0, 0, 1)
+        put("mul", a, 0)
+        put("sig", a, 1)
+        if j == 0:
+            put("c_x", 1)
+            put("c_decay", 0, 0, 1)
+        put("mm1", a, 2)
+        put("mul", a, 1)
+        if j == 0:
+            put("q_x", 1)
+        put("sig", a, 2)
+        put("mm1", a, 3)
+        put("mul", a, 2)
+        put("sig", a, 3)
+        put("mul", a, 3)
+        put("c_y", j - 4, 1)
+        put("cast", j - 3, 2)
+        put("mm2", b, 0)
+        put("sub", b, 0)
+        put("cast", b, 0)
+        put("mm2", b, 1)
+        put("sub", b, 1)
+        put("cast", b, 1)
+        put("dl", j - 1, 1, 2)
+        put("q_y", j - 4, 0, 1, 2)
+        put("planes", j - 4)
+        put("mm2", b, 2)
+        if b == last:
+            put("sub16", b, 2)
+        put("sub", b, 2)
+        hs = {0: [], 1: [0], 2: [1, 2]}.get(j, [j])
+        for h in hs:
+            put("t_h", h, 0, 1)
+        put("t_x", j + 2)
+        put("t_y", j - 3, 0, 1)
+        for h in hs:
+            put("c_h", h, 0, 1)
+            put("q_h", h, 0, 1)
+    put("t_y", last, 0, 1)
+    put("c_y", last - 1, 0, 1)
+    put("q_y", last - 1, 0, 1, 2)
+    put("planes", last - 1)
+    put("c_y", last, 0, 1)
+    put("q_y", last, 0, 1, 2)
+    put("planes", last)
+    return order
+
+
+def tile_regulated_protein_rates_h1_kernel(
+    tc, x, w_words, w_scales, rate, t_words, t_scales, decay, level, out_0, out_1, out_2
+):
+    nc = tc.nc
+    with ExitStack() as ctx:
+        keep = ctx.enter_context(tc.tile_pool(name="keep", bufs=1))
+        work = ctx.enter_context(tc.tile_pool(name="work", bufs=3))
+        psum = ctx.enter_context(tc.psum_pool(name="psum", bufs=1))
+        ctx.enter_context(tc.manual_schedule())
+
+        ident = keep.tile([P, P], F32, name="ident")
+        w_plane = keep.tile([P, RG, G], U8, name="w_plane", align_bytes=64)
+        t_plane = keep.tile([P, GG, N], U8, name="t_plane", align_bytes=64)
+        w_sb = keep.tile([P, RG, 2 * G], U8, name="w_sb", align_bytes=64)
+        t_sb = keep.tile([P, GG, 2 * N], U8, name="t_sb", align_bytes=64)
+        rate_p = keep.tile([P, GG, 4], BF16, name="rate_p")
+        decay_p = keep.tile([P, NG, 4], BF16, name="decay_p")
+        rate_all = keep.tile([P, GG, KP], BF16, name="rate_all")
+        decay_all = keep.tile([P, NG, KP], BF16, name="decay_all")
+        x_sb = [keep.tile([P, R], BF16, name="x%d" % i) for i in range(TILES)]
+        level_sb = [keep.tile([P, N], BF16, name="level%d" % i) for i in range(TILES)]
+        y_codes = keep.tile([P, NG, S], U32, name="y_codes", align_bytes=64)
+        y_scales = keep.tile([P, NG, S], U8, name="y_scales", align_bytes=64)
+        warm = keep.tile([P, 8], F32, name="warm")
+        warm_out = keep.tile([P, 8], F32, name="warm_out")
+
+        nc.vector.memset(w_plane[:].rearrange("p g n -> p (g n)").bitcast(I32), 0)
+        nc.vector.memset(warm[:], 0.0)
+        nc.scalar.activation(out=warm_out[:], in_=warm[:], func=ACT.Sigmoid)
+        make_identity(nc, ident[:])
+        nc.vector.memset(t_plane[:].rearrange("p g n -> p (g n)").bitcast(I32), 0)
+
+        def load_rows(dst, src, i):
+            nc.sync.dma_start(out=dst[i][:], in_=src[i * P:(i + 1) * P, :])
+
+        def load_scales(plane, scales):
+            for q in range(4):
+                nc.sync.dma_start(
+                    out=plane[32 * q:32 * q + 4, :, :].bitcast(I32),
+                    in_=scales[:, 4 * q:4 * q + 4, :].rearrange("g r n -> r g n").bitcast(I32),
+                )
+
+        def load_words(dst, words, c):
+            cols = slice(2 * KP * c, 2 * KP * (c + 1))
+            nc.sync.dma_start(
+                out=dst[:, :, cols].bitcast(I32),
+                in_=words[:, :, cols].rearrange("g p n -> p g n").bitcast(I32),
+            )
+
+        load_rows(x_sb, x, 0)
+        nc.sync.dma_start(out=rate_p[:], in_=rate.rearrange("(g m j) -> m g j", g=GG, j=4))
+        nc.sync.dma_start(out=decay_p[:], in_=decay.rearrange("(g m j) -> m g j", g=NG, j=4))
+        load_scales(w_plane, w_scales)
+        load_words(w_sb, w_words, 0)
+        load_words(w_sb, w_words, 1)
+        load_rows(x_sb, x, 1)
+        load_words(w_sb, w_words, 2)
+        load_words(w_sb, w_words, 3)
+        load_rows(x_sb, x, 2)
+        load_rows(level_sb, level, 0)
+        load_scales(t_plane, t_scales)
+        load_rows(x_sb, x, 3)
+        load_words(t_sb, t_words, 0)
+        load_rows(level_sb, level, 1)
+        load_words(t_sb, t_words, 1)
+        load_words(t_sb, t_words, 2)
+        for i in range(2, TILES):
+            if i + 2 < TILES:
+                load_rows(x_sb, x, i + 2)
+            load_rows(level_sb, level, i)
+
+        live = {}
+        used = []
+
+        def new_bank(key):
+            tag = "bank%d" % (len(used) % BANKS)
+            used.append(key)
+            live[key] = psum.tile([P, 4, P], F32, name=tag, tag=tag)
+            return live[key]
+
+        def flat(bank):
+            return bank[:].rearrange("p a b -> p (a b)")
+
+        def tile_of(kind, i, shape, dtype, bufs):
+            if (kind, i) not in live:
+                live[(kind, i)] = work.tile(shape, dtype, name=kind, tag=kind, bufs=bufs, align_bytes=64)
+            return live[(kind, i)]
+
+        def spread(kind, src, groups, b):
+            bank = new_bank((kind, b))
+            words = src[:].rearrange("p g j -> p (g j)").bitcast(F32)
+            for s in range(min(4, 2 * groups - 4 * b)):
+                col = 4 * b + s
+                nc.tensor.transpose(bank[:, s, :], words[:, col:col + 1].to_broadcast([P, P]), ident[:])
+
+        def t_rate(i, b):
+            spread("rate", rate_p, GG, b)
+
+        def t_decay(i, b):
+            spread("decay", decay_p, NG, b)
+
+        def c_rate(i, b):
+            dst = rate_all[:, 2 * b:2 * b + 2, :].rearrange("p g n -> p (g n)").bitcast(F32)
+            nc.vector.tensor_copy(out=dst, in_=flat(live[("rate", b)]))
+
+        def copy_out(eng, dst, bank, groups):
+            src = bank[:, :2 * groups, :].rearrange("p (g u) s -> p g s u", u=2)
+            dst = dst.bitcast(F32).rearrange("p g (s u) -> p g s u", u=2)
+            if eng == "scalar":
+                nc.scalar.copy(out=dst, in_=src)
+            else:
+                nc.vector.tensor_copy(out=dst, in_=src)
+
+        def c_decay(i, b):
+            n = min(2, NG - 2 * b)
+            copy_out("scalar", decay_all[:, 2 * b:2 * b + n, :], live[("decay", b)], n)
+
+        def t_x(i, k):
+            bank = new_bank(("tx", i))
+            words = x_sb[i][:].bitcast(F32)
+            for g in range(RG):
+                for u in range(2):
+                    nc.tensor.transpose(bank[:, 2 * g + u, :], words[:, 256 * g + u:256 * (g + 1):2], ident[:])
+
+        def c_x(i, k):
+            xt = tile_of("xt", i, [P, RG, KP], BF16, 2)
+            copy_out("scalar", xt[:], live[("tx", i)], RG)
+
+        def q_x(i, k):
+            codes = tile_of("xq", i, [P, RG * P], U32, 3)
+            scales = tile_of("xs", i, [P, RG * P], U8, 3)
+            nc.vector.quantize_mx(
+                out=codes[:].bitcast(FP8X4), scales=scales[:],
+                in_=live[("xt", i)][:].rearrange("p g n -> p (g n)"),
+            )
+
+        def product(bank, codes, scales, words, plane, groups, c):
+            for g in range(groups):
+                nc.tensor.matmul_mx(
+                    out=flat(bank),
+                    lhsT=codes[:, g * P:(g + 1) * P].bitcast(FP8X4),
+                    lhsT_scale=scales[:, g * P:(g + 1) * P],
+                    rhs=words[:, g, 2 * KP * c:2 * KP * (c + 1)].bitcast(FP4X4),
+                    rhs_scale=plane[:, g, KP * c:KP * (c + 1)],
+                    start=(g == 0),
+                    stop=(g == groups - 1),
+                )
+
+        def by_half(ap):
+            return ap.rearrange("p (m u e) -> p u m e", u=2, e=2)
+
+        def halves(ap):
+            return ap.rearrange("p (u m e) -> p u m e", u=2, e=2)
+
+        def mm1(i, c):
+            product(new_bank(("z", i, c)), live[("xq", i)], live[("xs", i)], w_sb, w_plane, RG, c)
+
+        def sig(i, c):
+            sg = tile_of("sg", (i, c), [P, KP], F32, 4)
+            nc.scalar.activation(out=halves(sg[:]), in_=by_half(flat(live[("z", i, c)])), func=ACT.Sigmoid)
+
+        def mul(i, c):
+            hb = tile_of("hb", i, [P, GG, KP], BF16, 3)
+            nc.vector.tensor_tensor(out=hb[:, c, :], in0=live[("sg", (i, c))][:], in1=rate_all[:, c, :], op=ALU.mult)
+
+        def turn(key, src, first, groups):
+            bank = new_bank(key)
+            for g in range(groups):
+                words = src[:, first + g, :].bitcast(F32)
+                for u in range(2):
+                    nc.tensor.transpose(bank[:, 2 * g + u, :], words[:, P * u:P * (u + 1)], ident[:])
+
+        def t_h(i, b):
+            turn(("th", i, b), live[("hb", i)], 2 * b, 2)
+
+        def c_h(i, b):
+            ht = tile_of("ht", i, [P, GG, KP], BF16, 3)
+            copy_out("scalar", ht[:, 2 * b:2 * b + 2, :], live[("th", i, b)], 2)
+
+        def q_h(i, b):
+            codes = tile_of("hq", i, [P, GG * P], U32, 4)
+            scales = tile_of("hs", i, [P, GG * P], U8, 4)
+            cols = slice(2 * P * b, 2 * P * (b + 1))
+            nc.vector.quantize_mx(
+                out=codes[:, cols].bitcast(FP8X4), scales=scales[:, cols],
+                in_=live[("ht", i)][:, 2 * b:2 * b + 2, :].rearrange("p g n -> p (g n)"),
+            )
+
+        def mm2(i, n):
+            product(new_bank(("acc", i, n)), live[("hq", i)], live[("hs", i)], t_sb, t_plane, GG, n)
+
+        def dl(i, n):
+            loss = tile_of("loss", (i, n), [P, KP], F32, 6)
+            nc.vector.tensor_tensor(
+                out=loss[:], in0=level_sb[i][:, KP * n:KP * (n + 1)], in1=decay_all[:, n, :], op=ALU.mult
+            )
+
+        def sub(i, n):
+            y = tile_of("y", (i, n), [P, KP], F32, 6)
+            nc.vector.tensor_tensor(
+                out=y[:], in0=flat(live[("acc", i, n)]), in1=live[("loss", (i, n))][:], op=ALU.subtract
+            )
+            nc.sync.dma_start(out=out_0[i * P:(i + 1) * P, KP * n:KP * (n + 1)], in_=y[:])
+
+        def sub16(i, n):
+            yb = tile_of("yb", i, [P, NG, KP], BF16, 3)
+            nc.vector.tensor_tensor(
+                out=halves(yb[:, n, :]), in0=by_half(flat(live[("acc", i, n)])),
+                in1=by_half(live[("loss", (i, n))][:]), op=ALU.subtract,
+            )
+
+        def cast(i, n):
+            yb = tile_of("yb", i, [P, NG, KP], BF16, 3)
+            nc.scalar.copy(out=halves(yb[:, n, :]), in_=by_half(live[("y", (i, n))][:]))
+
+        def t_y(i, b):
+            turn(("ty", i, b), live[("yb", i)], 2 * b, min(2, NG - 2 * b))
+
+        def c_y(i, b):
+            yt = tile_of("yt", i, [P, NG, KP], BF16, 2)
+            n = min(2, NG - 2 * b)
+            copy_out("scalar", yt[:, 2 * b:2 * b + n, :], live[("ty", i, b)], n)
+
+        def q_y(i, g):
+            cols = slice(i * P, (i + 1) * P)
+            nc.vector.quantize_mx(
+                out=y_codes[:, g, cols].bitcast(FP8X4), scales=y_scales[:, g, cols], in_=live[("yt", i)][:, g, :]
+            )
+
+        words_out = out_1.rearrange("g p m t -> p g (m t)").bitcast(I32)
+
+        def planes(i, k):
+            first = {3: 0, 4: 4, 5: 5}.get(i)
+            if first is not None:
+                cols = slice(first * P, (i + 1) * P)
+                nc.sync.dma_start(out=words_out[:, :, cols], in_=y_codes[:, :, cols].bitcast(I32))
+            first = {4: 0, 5: 5}.get(i)
+            if first is not None:
+                cols = slice(first * P, (i + 1) * P)
+                for q in range(4):
+                    eng = nc.scalar if (i == TILES - 1 and q % 2) else nc.sync
+                    eng.dma_start(
+                        out=out_2[:, 4 * q:4 * q + 4, cols].rearrange("g r m -> r g m").bitcast(I32),
+                        in_=y_scales[32 * q:32 * q + 4, :, cols].bitcast(I32),
+                    )
+
+        steps = {
+            "t_rate": t_rate, "t_decay": t_decay, "c_rate": c_rate, "c_decay": c_decay,
+            "t_x": t_x, "c_x": c_x, "q_x": q_x, "mm1": mm1, "sig": sig, "mul": mul,
+            "t_h": t_h, "c_h": c_h, "q_h": q_h, "mm2": mm2, "dl": dl, "sub": sub, "sub16": sub16,
+            "cast": cast, "t_y": t_y, "c_y": c_y, "q_y": q_y, "planes": planes,
+        }
+        for name, i, k in schedule():
+            steps[name](i, k)

@@ -31,68 +31,83 @@ def schedule():
             order.extend((name, i, k) for k in (ks or (0,)))
 
     last = TILES - 1
+    put("t_vec", 0)
     put("t_x", 0)
-    put("t_rate", 0, 0, 1)
+    put("c_vec", 0)
+    put("t_rate", 0, 0)
+    put("t_decay", 0, 0)
     put("c_x", 0)
     put("q_x", 0)
-    put("c_rate", 0, 0, 1)
+    put("c_rate", 0, 0)
+    put("c_decay", 0, 0)
     for j in range(TILES + 2):
         a, b = j, j - 2
+        turned_h = {0: [], 1: [0], 2: [1, 2]}.get(j, [j])
         put("mm1", a, 0)
         if j > 0:
             put("c_x", j + 1)
             put("q_x", j + 1)
-        put("c_y", j - 4, 0)
-        put("dl", j - 1, 0)
+        put("c_y", j - 4, 0, 1)
         put("sig", a, 0)
         put("mm1", a, 1)
         if j == 0:
             put("t_x", 1)
-            put("t_decay", 0, 0, 1)
-        put("mul", a, 0)
+            put("t_rate", 0, 1)
+            put("t_decay", 0, 1)
         put("sig", a, 1)
+        put("mul", a, 0)
         if j == 0:
             put("c_x", 1)
-            put("c_decay", 0, 0, 1)
+            put("c_rate", 0, 1)
+            put("c_decay", 0, 1)
         put("mm1", a, 2)
-        put("mul", a, 1)
         if j == 0:
             put("q_x", 1)
+            put("dl", 0)
         put("sig", a, 2)
         put("mm1", a, 3)
-        put("mul", a, 2)
         put("sig", a, 3)
-        put("mul", a, 3)
-        put("c_y", j - 4, 1)
-        put("cast", j - 3, 2)
+        put("mul", a, 1)
+        if j == 7:
+            put("cast", 4, 2)
         put("mm2", b, 0)
         put("sub", b, 0)
-        put("cast", b, 0)
+        if j - 3 < last - 1:
+            put("cast", j - 3)
         put("mm2", b, 1)
         put("sub", b, 1)
-        put("cast", b, 1)
-        put("dl", j - 1, 1, 2)
-        put("q_y", j - 4, 0, 1, 2)
-        put("planes", j - 4)
+        if b >= last - 1:
+            put("cast", b, 1)
+        if j == 6:
+            put("q_y", 1, 0, 1, 2)
+            put("codes", 1, 2)
+        if j == 7:
+            put("q_y", 3, 0, 1, 2)
+            put("codes", 3, 2)
+            put("scales", 3)
         put("mm2", b, 2)
         if b == last:
             put("sub16", b, 2)
         put("sub", b, 2)
-        hs = {0: [], 1: [0], 2: [1, 2]}.get(j, [j])
-        for h in hs:
+        for h in turned_h:
             put("t_h", h, 0, 1)
         put("t_x", j + 2)
         put("t_y", j - 3, 0, 1)
-        for h in hs:
+        for h in turned_h:
             put("c_h", h, 0, 1)
-            put("q_h", h, 0, 1)
+            put("q_h", h)
+        if j > 0:
+            put("dl", j)
     put("t_y", last, 0, 1)
-    put("c_y", last - 1, 0, 1)
-    put("q_y", last - 1, 0, 1, 2)
-    put("planes", last - 1)
-    put("c_y", last, 0, 1)
-    put("q_y", last, 0, 1, 2)
-    put("planes", last)
+    put("c_y", last - 1, 0)
+    put("c_y", last, 0)
+    put("c_y", last - 1, 1)
+    put("c_y", last, 1)
+    put("q_y", last, 0, 1)
+    put("codes", last, 0)
+    put("q_y", last, 2)
+    put("codes", last, 1)
+    put("scales", last)
     return order
 
 
@@ -111,31 +126,41 @@ def tile_regulated_protein_rates_h1_kernel(
         t_plane = keep.tile([P, GG, N], U8, name="t_plane", align_bytes=64)
         w_sb = keep.tile([P, RG, 2 * G], U8, name="w_sb", align_bytes=64)
         t_sb = keep.tile([P, GG, 2 * N], U8, name="t_sb", align_bytes=64)
-        rate_p = keep.tile([P, GG, 4], BF16, name="rate_p")
-        decay_p = keep.tile([P, NG, 4], BF16, name="decay_p")
+        vec = keep.tile([P, KP], BF16, name="vec")
+        vec_p = keep.tile([P, 2, 8], F32, name="vec_p")
         rate_all = keep.tile([P, GG, KP], BF16, name="rate_all")
         decay_all = keep.tile([P, NG, KP], BF16, name="decay_all")
         x_sb = [keep.tile([P, R], BF16, name="x%d" % i) for i in range(TILES)]
         level_sb = [keep.tile([P, N], BF16, name="level%d" % i) for i in range(TILES)]
+        loss = [keep.tile([P, N], F32, name="loss%d" % i) for i in range(4)]
+        loss = [loss[i % 4] for i in range(TILES)]
+        y_sb = [keep.tile([P, N], F32, name="y%d" % i) for i in range(4)]
+        y_sb = [y_sb[i % 4] for i in range(TILES)]
+        y_bf = [keep.tile([P, 2, N // 2], BF16, name="yb%d" % i) for i in range(TILES)]
+        y_turned = keep.tile([P, NG, 4 * S], BF16, name="y_turned", align_bytes=64)
         y_codes = keep.tile([P, NG, S], U32, name="y_codes", align_bytes=64)
         y_scales = keep.tile([P, NG, S], U8, name="y_scales", align_bytes=64)
         warm = keep.tile([P, 8], F32, name="warm")
         warm_out = keep.tile([P, 8], F32, name="warm_out")
 
-        nc.vector.memset(w_plane[:].rearrange("p g n -> p (g n)").bitcast(I32), 0)
+        nc.vector.memset(vec[:].bitcast(I32), 0)
+        nc.vector.memset(w_plane[:, :, :G // 2].bitcast(I32), 0)
         nc.vector.memset(warm[:], 0.0)
+        nc.scalar.dma_start(out=vec[0:GG, :], in_=rate.rearrange("(g n) -> g n", g=GG))
+        nc.scalar.dma_start(out=vec[GG:GG + NG, :], in_=decay.rearrange("(g n) -> g n", g=NG))
         nc.scalar.activation(out=warm_out[:], in_=warm[:], func=ACT.Sigmoid)
         make_identity(nc, ident[:])
+        nc.vector.memset(w_plane[:, :, G // 2:].bitcast(I32), 0)
         nc.vector.memset(t_plane[:].rearrange("p g n -> p (g n)").bitcast(I32), 0)
 
         def load_rows(dst, src, i):
             nc.sync.dma_start(out=dst[i][:], in_=src[i * P:(i + 1) * P, :])
 
-        def load_scales(plane, scales):
+        def load_scales(plane, scales, cols):
             for q in range(4):
                 nc.sync.dma_start(
-                    out=plane[32 * q:32 * q + 4, :, :].bitcast(I32),
-                    in_=scales[:, 4 * q:4 * q + 4, :].rearrange("g r n -> r g n").bitcast(I32),
+                    out=plane[32 * q:32 * q + 4, :, cols].bitcast(I32),
+                    in_=scales[:, 4 * q:4 * q + 4, cols].rearrange("g r n -> r g n").bitcast(I32),
                 )
 
         def load_words(dst, words, c):
@@ -146,17 +171,16 @@ def tile_regulated_protein_rates_h1_kernel(
             )
 
         load_rows(x_sb, x, 0)
-        nc.sync.dma_start(out=rate_p[:], in_=rate.rearrange("(g m j) -> m g j", g=GG, j=4))
-        nc.sync.dma_start(out=decay_p[:], in_=decay.rearrange("(g m j) -> m g j", g=NG, j=4))
-        load_scales(w_plane, w_scales)
+        load_scales(w_plane, w_scales, slice(0, G // 2))
         load_words(w_sb, w_words, 0)
         load_words(w_sb, w_words, 1)
         load_rows(x_sb, x, 1)
+        load_rows(level_sb, level, 0)
+        load_scales(w_plane, w_scales, slice(G // 2, G))
         load_words(w_sb, w_words, 2)
         load_words(w_sb, w_words, 3)
         load_rows(x_sb, x, 2)
-        load_rows(level_sb, level, 0)
-        load_scales(t_plane, t_scales)
+        load_scales(t_plane, t_scales, slice(0, N))
         load_rows(x_sb, x, 3)
         load_words(t_sb, t_words, 0)
         load_rows(level_sb, level, 1)
@@ -184,22 +208,31 @@ def tile_regulated_protein_rates_h1_kernel(
                 live[(kind, i)] = work.tile(shape, dtype, name=kind, tag=kind, bufs=bufs, align_bytes=64)
             return live[(kind, i)]
 
-        def spread(kind, src, groups, b):
+        def t_vec(i, k):
+            bank = new_bank("vec")
+            words = vec[:].bitcast(F32)
+            for u in range(2):
+                nc.tensor.transpose(bank[:, u, :], words[:, u:256:2], ident[:])
+
+        def c_vec(i, k):
+            nc.vector.tensor_copy(out=vec_p[:], in_=live["vec"][:, 0:2, 0:8])
+
+        def spread(kind, row, groups, b):
             bank = new_bank((kind, b))
-            words = src[:].rearrange("p g j -> p (g j)").bitcast(F32)
-            for s in range(min(4, 2 * groups - 4 * b)):
-                col = 4 * b + s
-                nc.tensor.transpose(bank[:, s, :], words[:, col:col + 1].to_broadcast([P, P]), ident[:])
+            for g in range(min(2, groups - 2 * b)):
+                r = row + 2 * b + g
+                for u in range(2):
+                    nc.tensor.transpose(bank[:, 2 * g + u, :], vec_p[:, u, r:r + 1].to_broadcast([P, P]), ident[:])
 
         def t_rate(i, b):
-            spread("rate", rate_p, GG, b)
+            spread("rate", 0, GG, b)
 
         def t_decay(i, b):
-            spread("decay", decay_p, NG, b)
+            spread("decay", GG, NG, b)
 
         def c_rate(i, b):
             dst = rate_all[:, 2 * b:2 * b + 2, :].rearrange("p g n -> p (g n)").bitcast(F32)
-            nc.vector.tensor_copy(out=dst, in_=flat(live[("rate", b)]))
+            nc.scalar.copy(out=dst, in_=flat(live[("rate", b)]))
 
         def copy_out(eng, dst, bank, groups):
             src = bank[:, :2 * groups, :].rearrange("p (g u) s -> p g s u", u=2)
@@ -254,99 +287,101 @@ def tile_regulated_protein_rates_h1_kernel(
             product(new_bank(("z", i, c)), live[("xq", i)], live[("xs", i)], w_sb, w_plane, RG, c)
 
         def sig(i, c):
-            sg = tile_of("sg", (i, c), [P, KP], F32, 4)
-            nc.scalar.activation(out=halves(sg[:]), in_=by_half(flat(live[("z", i, c)])), func=ACT.Sigmoid)
+            sg = tile_of("sg", (i, c // 2), [P, 2, KP], F32, 3)
+            nc.scalar.activation(out=halves(sg[:, c % 2, :]), in_=by_half(flat(live[("z", i, c)])), func=ACT.Sigmoid)
 
-        def mul(i, c):
+        def mul(i, b):
             hb = tile_of("hb", i, [P, GG, KP], BF16, 3)
-            nc.vector.tensor_tensor(out=hb[:, c, :], in0=live[("sg", (i, c))][:], in1=rate_all[:, c, :], op=ALU.mult)
-
-        def turn(key, src, first, groups):
-            bank = new_bank(key)
-            for g in range(groups):
-                words = src[:, first + g, :].bitcast(F32)
-                for u in range(2):
-                    nc.tensor.transpose(bank[:, 2 * g + u, :], words[:, P * u:P * (u + 1)], ident[:])
+            pair = slice(2 * b, 2 * b + 2)
+            nc.vector.tensor_tensor(out=hb[:, pair, :], in0=live[("sg", (i, b))][:], in1=rate_all[:, pair, :], op=ALU.mult)
 
         def t_h(i, b):
-            turn(("th", i, b), live[("hb", i)], 2 * b, 2)
+            bank = new_bank(("th", i, b))
+            for g in range(2):
+                words = live[("hb", i)][:, 2 * b + g, :].bitcast(F32)
+                for u in range(2):
+                    nc.tensor.transpose(bank[:, 2 * g + u, :], words[:, P * u:P * (u + 1)], ident[:])
 
         def c_h(i, b):
             ht = tile_of("ht", i, [P, GG, KP], BF16, 3)
             copy_out("scalar", ht[:, 2 * b:2 * b + 2, :], live[("th", i, b)], 2)
 
-        def q_h(i, b):
+        def q_h(i, k):
             codes = tile_of("hq", i, [P, GG * P], U32, 4)
             scales = tile_of("hs", i, [P, GG * P], U8, 4)
-            cols = slice(2 * P * b, 2 * P * (b + 1))
             nc.vector.quantize_mx(
-                out=codes[:, cols].bitcast(FP8X4), scales=scales[:, cols],
-                in_=live[("ht", i)][:, 2 * b:2 * b + 2, :].rearrange("p g n -> p (g n)"),
+                out=codes[:].bitcast(FP8X4), scales=scales[:],
+                in_=live[("ht", i)][:].rearrange("p g n -> p (g n)"),
             )
 
         def mm2(i, n):
             product(new_bank(("acc", i, n)), live[("hq", i)], live[("hs", i)], t_sb, t_plane, GG, n)
 
-        def dl(i, n):
-            loss = tile_of("loss", (i, n), [P, KP], F32, 6)
+        def dl(i, k):
             nc.vector.tensor_tensor(
-                out=loss[:], in0=level_sb[i][:, KP * n:KP * (n + 1)], in1=decay_all[:, n, :], op=ALU.mult
+                out=loss[i][:], in0=level_sb[i][:], in1=decay_all[:].rearrange("p g n -> p (g n)"), op=ALU.mult
             )
 
         def sub(i, n):
-            y = tile_of("y", (i, n), [P, KP], F32, 6)
+            cols = slice(KP * n, KP * (n + 1))
             nc.vector.tensor_tensor(
-                out=y[:], in0=flat(live[("acc", i, n)]), in1=live[("loss", (i, n))][:], op=ALU.subtract
+                out=y_sb[i][:, cols], in0=flat(live[("acc", i, n)]), in1=loss[i][:, cols], op=ALU.subtract
             )
-            nc.sync.dma_start(out=out_0[i * P:(i + 1) * P, KP * n:KP * (n + 1)], in_=y[:])
+            nc.sync.dma_start(out=out_0[i * P:(i + 1) * P, cols], in_=y_sb[i][:, cols])
+
+        def rounded(i, first, stop):
+            return y_bf[i][:].rearrange("p u (m e) -> p u m e", e=2)[:, :, P * first:P * stop, :]
 
         def sub16(i, n):
-            yb = tile_of("yb", i, [P, NG, KP], BF16, 3)
             nc.vector.tensor_tensor(
-                out=halves(yb[:, n, :]), in0=by_half(flat(live[("acc", i, n)])),
-                in1=by_half(live[("loss", (i, n))][:]), op=ALU.subtract,
+                out=rounded(i, n, n + 1), in0=by_half(flat(live[("acc", i, n)])),
+                in1=by_half(loss[i][:, KP * n:KP * (n + 1)]), op=ALU.subtract,
             )
 
-        def cast(i, n):
-            yb = tile_of("yb", i, [P, NG, KP], BF16, 3)
-            nc.scalar.copy(out=halves(yb[:, n, :]), in_=by_half(live[("y", (i, n))][:]))
+        def cast(i, k):
+            first, stop = ((0, NG), (0, 2), (2, NG))[k]
+            nc.scalar.copy(out=rounded(i, first, stop), in_=by_half(y_sb[i][:, KP * first:KP * stop]))
 
         def t_y(i, b):
-            turn(("ty", i, b), live[("yb", i)], 2 * b, min(2, NG - 2 * b))
+            bank = new_bank(("ty", i, b))
+            words = y_bf[i][:].bitcast(F32)
+            for g in range(min(2, NG - 2 * b)):
+                first = P * (2 * b + g)
+                for u in range(2):
+                    nc.tensor.transpose(bank[:, 2 * g + u, :], words[:, u, first:first + P], ident[:])
 
         def c_y(i, b):
-            yt = tile_of("yt", i, [P, NG, KP], BF16, 2)
             n = min(2, NG - 2 * b)
-            copy_out("scalar", yt[:, 2 * b:2 * b + n, :], live[("ty", i, b)], n)
+            copy_out("scalar", y_turned[:, 2 * b:2 * b + n, KP * i:KP * (i + 1)], live[("ty", i, b)], n)
 
         def q_y(i, g):
-            cols = slice(i * P, (i + 1) * P)
+            cols = slice((i - 1) * P, (i + 1) * P)
             nc.vector.quantize_mx(
-                out=y_codes[:, g, cols].bitcast(FP8X4), scales=y_scales[:, g, cols], in_=live[("yt", i)][:, g, :]
+                out=y_codes[:, g, cols].bitcast(FP8X4), scales=y_scales[:, g, cols],
+                in_=y_turned[:, g, KP * (i - 1):KP * (i + 1)],
             )
 
         words_out = out_1.rearrange("g p m t -> p g (m t)").bitcast(I32)
 
-        def planes(i, k):
-            first = {3: 0, 4: 4, 5: 5}.get(i)
-            if first is not None:
-                cols = slice(first * P, (i + 1) * P)
-                nc.sync.dma_start(out=words_out[:, :, cols], in_=y_codes[:, :, cols].bitcast(I32))
-            first = {4: 0, 5: 5}.get(i)
-            if first is not None:
-                cols = slice(first * P, (i + 1) * P)
-                for q in range(4):
-                    eng = nc.scalar if (i == TILES - 1 and q % 2) else nc.sync
-                    eng.dma_start(
-                        out=out_2[:, 4 * q:4 * q + 4, cols].rearrange("g r m -> r g m").bitcast(I32),
-                        in_=y_scales[32 * q:32 * q + 4, :, cols].bitcast(I32),
-                    )
+        def codes_out(i, k):
+            groups = (slice(0, 2), slice(2, NG), slice(0, NG))[k]
+            cols = slice((i - 1) * P, (i + 1) * P)
+            nc.sync.dma_start(out=words_out[:, groups, cols], in_=y_codes[:, groups, cols].bitcast(I32))
+
+        def scales_out(i, k):
+            cols = slice(0, 4 * P) if i == 3 else slice(4 * P, S)
+            for q in range(4):
+                eng = nc.scalar if (i == TILES - 1 and q % 2) else nc.sync
+                eng.dma_start(
+                    out=out_2[:, 4 * q:4 * q + 4, cols].rearrange("g r m -> r g m").bitcast(I32),
+                    in_=y_scales[32 * q:32 * q + 4, :, cols].bitcast(I32),
+                )
 
         steps = {
-            "t_rate": t_rate, "t_decay": t_decay, "c_rate": c_rate, "c_decay": c_decay,
+            "t_vec": t_vec, "c_vec": c_vec, "t_rate": t_rate, "t_decay": t_decay, "c_rate": c_rate, "c_decay": c_decay,
             "t_x": t_x, "c_x": c_x, "q_x": q_x, "mm1": mm1, "sig": sig, "mul": mul,
             "t_h": t_h, "c_h": c_h, "q_h": q_h, "mm2": mm2, "dl": dl, "sub": sub, "sub16": sub16,
-            "cast": cast, "t_y": t_y, "c_y": c_y, "q_y": q_y, "planes": planes,
+            "cast": cast, "t_y": t_y, "c_y": c_y, "q_y": q_y, "codes": codes_out, "scales": scales_out,
         }
         for name, i, k in schedule():
             steps[name](i, k)

@@ -23,92 +23,46 @@ RG, GG, NG = R // KP, G // KP, N // KP
 BANKS = 8
 
 
-def schedule():
-    order = []
+ORDER = """
+t_vec t_x c_vec
+t_decay c_x* t_decay t_rate q_x mm1 c_rate* c_decay* c_decay t_x t_rate dl
+c_x mm1 sig q_x mm1 sig c_rate* mm1 sig t_x mul sig mm1
+c_x mm1 mul sig mm1 mm1 sig q_x t_x dl sig t_h c_x t_h mm1 sig mul mm1
+sig mm1 q_x c_h mm1 mul c_h mm1 mm1 sig q_h t_x sig mul t_h sig t_h
+mm1 sig dl mm2 sig c_x mm2 mul c_h c_h mm1 sub mm2 sig
+q_x sig mul mm1 t_h sig sub t_h t_x c_h q_h mm1 c_x mul mm2 c_h
+sub mm2 dl cast mm1 mm2 q_x sig sub mm1 sig sub
+t_y t_h q_h c_y t_y t_h sub mm1 c_h dl mm1 sig mm2 c_h cast mul mm2
+mm1 mul c_y mm1 sig mm2 q_h sig sub sig t_y sub t_h sig
+t_h sub mm2 c_h mul c_y mm2 c_h sub cast mm2 mul t_h
+q_h t_h c_h t_y sub mm2 c_y sub c_h dl mm2 cast mm2 sub
+q_h t_y t_y t_y q_y c_y mm2 sub c_y q_y cast q_y mm2 sub c_y sub
+t_y t_y cast mm2 sub c_y q_y c_y cast* t_y codes q_y c_y t_y q_y sub16 c_y scales codes
+sub t_y q_y c_y q_y q_y codes codes scales
+"""
 
-    def put(name, i, *ks):
-        if 0 <= i < TILES:
-            order.extend((name, i, k) for k in (ks or (0,)))
 
-    last = TILES - 1
-    put("t_vec", 0)
-    put("t_x", 0)
-    put("c_vec", 0)
-    put("t_rate", 0, 0)
-    put("t_decay", 0, 0)
-    put("c_x", 0)
-    put("q_x", 0)
-    put("c_rate", 0, 0)
-    put("c_decay", 0, 0)
-    for j in range(TILES + 2):
-        a, b = j, j - 2
-        turned_h = {0: [], 1: [0], 2: [1, 2]}.get(j, [j])
-        put("mm1", a, 0)
-        if j > 0:
-            put("c_x", j + 1)
-            put("q_x", j + 1)
-        put("c_y", j - 4, 0, 1)
-        put("sig", a, 0)
-        put("mm1", a, 1)
-        if j == 0:
-            put("t_x", 1)
-            put("t_rate", 0, 1)
-            put("t_decay", 0, 1)
-        put("sig", a, 1)
-        put("mul", a, 0)
-        if j == 0:
-            put("c_x", 1)
-            put("c_rate", 0, 1)
-            put("c_decay", 0, 1)
-        put("mm1", a, 2)
-        if j == 0:
-            put("q_x", 1)
-            put("dl", 0)
-        put("sig", a, 2)
-        put("mm1", a, 3)
-        put("sig", a, 3)
-        put("mul", a, 1)
-        if j == 7:
-            put("cast", 4, 2)
-        put("mm2", b, 0)
-        put("sub", b, 0)
-        if j - 3 < last - 1:
-            put("cast", j - 3)
-        put("mm2", b, 1)
-        put("sub", b, 1)
-        if b >= last - 1:
-            put("cast", b, 1)
-        if j == 6:
-            put("q_y", 1, 0, 1, 2)
-            put("codes", 1, 2)
-        if j == 7:
-            put("q_y", 3, 0, 1, 2)
-            put("codes", 3, 2)
-            put("scales", 3)
-        put("mm2", b, 2)
-        if b == last:
-            put("sub16", b, 2)
-        put("sub", b, 2)
-        for h in turned_h:
-            put("t_h", h, 0, 1)
-        put("t_x", j + 2)
-        put("t_y", j - 3, 0, 1)
-        for h in turned_h:
-            put("c_h", h, 0, 1)
-            put("q_h", h)
-        if j > 0:
-            put("dl", j)
-    put("t_y", last, 0, 1)
-    put("c_y", last - 1, 0)
-    put("c_y", last, 0)
-    put("c_y", last - 1, 1)
-    put("c_y", last, 1)
-    put("q_y", last, 0, 1)
-    put("codes", last, 0)
-    put("q_y", last, 2)
-    put("codes", last, 1)
-    put("scales", last)
-    return order
+def pieces():
+    tiles = range(TILES)
+    table = {}
+    for kinds, per_tile in (
+        (("t_x", "c_x", "q_x", "q_h", "dl"), 1),
+        (("mul", "t_h", "c_h", "t_y", "c_y"), 2),
+        (("mm2", "sub"), NG),
+        (("mm1", "sig"), GG),
+    ):
+        for kind in kinds:
+            table[kind] = [(i, k) for i in tiles for k in range(per_tile)]
+    for kind in ("t_rate", "c_rate", "t_decay", "c_decay"):
+        table[kind] = [(0, 0), (0, 1)]
+    for kind in ("t_vec", "c_vec"):
+        table[kind] = [(0, 0)]
+    table["cast"] = [(0, 0), (1, 0), (2, 0), (3, 0), (4, 1), (4, 2), (5, 1)]
+    table["sub16"] = [(5, 2)]
+    table["q_y"] = [(i, g) for i in (1, 3, 5) for g in range(NG)]
+    table["codes"] = [(1, 2), (3, 2), (5, 0), (5, 1)]
+    table["scales"] = [(3, 0), (5, 0)]
+    return table
 
 
 def tile_regulated_protein_rates_h1_kernel(
@@ -122,10 +76,10 @@ def tile_regulated_protein_rates_h1_kernel(
         ctx.enter_context(tc.manual_schedule())
 
         ident = keep.tile([P, P], F32, name="ident")
-        w_plane = keep.tile([P, RG, G], U8, name="w_plane", align_bytes=64)
-        t_plane = keep.tile([P, GG, N], U8, name="t_plane", align_bytes=64)
-        w_sb = keep.tile([P, RG, 2 * G], U8, name="w_sb", align_bytes=64)
-        t_sb = keep.tile([P, GG, 2 * N], U8, name="t_sb", align_bytes=64)
+        w_plane = keep.tile([P, RG, G], U8, name="w_plane", align_bytes=256)
+        t_plane = keep.tile([P, GG, N], U8, name="t_plane", align_bytes=256)
+        w_sb = keep.tile([P, RG, 2 * G], U8, name="w_sb", align_bytes=256)
+        t_sb = keep.tile([P, GG, 2 * N], U8, name="t_sb", align_bytes=256)
         vec = keep.tile([P, KP], BF16, name="vec")
         vec_p = keep.tile([P, 2, 8], F32, name="vec_p")
         rate_all = keep.tile([P, GG, KP], BF16, name="rate_all")
@@ -137,13 +91,13 @@ def tile_regulated_protein_rates_h1_kernel(
         y_sb = [keep.tile([P, N], F32, name="y%d" % i) for i in range(4)]
         y_sb = [y_sb[i % 4] for i in range(TILES)]
         y_bf = [keep.tile([P, 2, N // 2], BF16, name="yb%d" % i) for i in range(TILES)]
-        y_turned = keep.tile([P, NG, 4 * S], BF16, name="y_turned", align_bytes=64)
-        y_codes = keep.tile([P, NG, S], U32, name="y_codes", align_bytes=64)
-        y_scales = keep.tile([P, NG, S], U8, name="y_scales", align_bytes=64)
+        y_turned = keep.tile([P, NG, 4 * S], BF16, name="y_turned", align_bytes=256)
+        y_codes = keep.tile([P, NG, S], U32, name="y_codes", align_bytes=256)
+        y_scales = keep.tile([P, NG, S], U8, name="y_scales", align_bytes=256)
         warm = keep.tile([P, 8], F32, name="warm")
         warm_out = keep.tile([P, 8], F32, name="warm_out")
 
-        nc.vector.memset(vec[:].bitcast(I32), 0)
+        nc.gpsimd.memset(vec[:].bitcast(I32), 0)
         nc.vector.memset(w_plane[:, :, :G // 2].bitcast(I32), 0)
         nc.vector.memset(warm[:], 0.0)
         nc.scalar.dma_start(out=vec[0:GG, :], in_=rate.rearrange("(g n) -> g n", g=GG))
@@ -176,6 +130,7 @@ def tile_regulated_protein_rates_h1_kernel(
         load_words(w_sb, w_words, 1)
         load_rows(x_sb, x, 1)
         load_rows(level_sb, level, 0)
+        load_rows(level_sb, level, 1)
         load_scales(w_plane, w_scales, slice(G // 2, G))
         load_words(w_sb, w_words, 2)
         load_words(w_sb, w_words, 3)
@@ -183,13 +138,14 @@ def tile_regulated_protein_rates_h1_kernel(
         load_scales(t_plane, t_scales, slice(0, N))
         load_rows(x_sb, x, 3)
         load_words(t_sb, t_words, 0)
-        load_rows(level_sb, level, 1)
         load_words(t_sb, t_words, 1)
+        load_rows(level_sb, level, 2)
         load_words(t_sb, t_words, 2)
-        for i in range(2, TILES):
-            if i + 2 < TILES:
-                load_rows(x_sb, x, i + 2)
-            load_rows(level_sb, level, i)
+        load_rows(x_sb, x, 4)
+        load_rows(level_sb, level, 3)
+        load_rows(x_sb, x, 5)
+        load_rows(level_sb, level, 4)
+        load_rows(level_sb, level, 5)
 
         live = {}
         used = []
@@ -205,8 +161,14 @@ def tile_regulated_protein_rates_h1_kernel(
 
         def tile_of(kind, i, shape, dtype, bufs):
             if (kind, i) not in live:
-                live[(kind, i)] = work.tile(shape, dtype, name=kind, tag=kind, bufs=bufs, align_bytes=64)
+                live[(kind, i)] = work.tile(shape, dtype, name=kind, tag=kind, bufs=bufs, align_bytes=256)
             return live[(kind, i)]
+
+        def copy(on_vector, dst, src):
+            if on_vector:
+                nc.vector.tensor_copy(out=dst, in_=src)
+            else:
+                nc.scalar.copy(out=dst, in_=src)
 
         def t_vec(i, k):
             bank = new_bank("vec")
@@ -230,21 +192,17 @@ def tile_regulated_protein_rates_h1_kernel(
         def t_decay(i, b):
             spread("decay", GG, NG, b)
 
-        def c_rate(i, b):
+        def c_rate(i, b, on_vector=False):
             dst = rate_all[:, 2 * b:2 * b + 2, :].rearrange("p g n -> p (g n)").bitcast(F32)
-            nc.scalar.copy(out=dst, in_=flat(live[("rate", b)]))
+            copy(on_vector, dst, flat(live[("rate", b)]))
 
-        def copy_out(eng, dst, bank, groups):
+        def copy_out(on_vector, dst, bank, groups):
             src = bank[:, :2 * groups, :].rearrange("p (g u) s -> p g s u", u=2)
-            dst = dst.bitcast(F32).rearrange("p g (s u) -> p g s u", u=2)
-            if eng == "scalar":
-                nc.scalar.copy(out=dst, in_=src)
-            else:
-                nc.vector.tensor_copy(out=dst, in_=src)
+            copy(on_vector, dst.bitcast(F32).rearrange("p g (s u) -> p g s u", u=2), src)
 
-        def c_decay(i, b):
+        def c_decay(i, b, on_vector=False):
             n = min(2, NG - 2 * b)
-            copy_out("scalar", decay_all[:, 2 * b:2 * b + n, :], live[("decay", b)], n)
+            copy_out(on_vector, decay_all[:, 2 * b:2 * b + n, :], live[("decay", b)], n)
 
         def t_x(i, k):
             bank = new_bank(("tx", i))
@@ -253,9 +211,9 @@ def tile_regulated_protein_rates_h1_kernel(
                 for u in range(2):
                     nc.tensor.transpose(bank[:, 2 * g + u, :], words[:, 256 * g + u:256 * (g + 1):2], ident[:])
 
-        def c_x(i, k):
+        def c_x(i, k, on_vector=False):
             xt = tile_of("xt", i, [P, RG, KP], BF16, 2)
-            copy_out("scalar", xt[:], live[("tx", i)], RG)
+            copy_out(on_vector, xt[:], live[("tx", i)], RG)
 
         def q_x(i, k):
             codes = tile_of("xq", i, [P, RG * P], U32, 3)
@@ -287,7 +245,7 @@ def tile_regulated_protein_rates_h1_kernel(
             product(new_bank(("z", i, c)), live[("xq", i)], live[("xs", i)], w_sb, w_plane, RG, c)
 
         def sig(i, c):
-            sg = tile_of("sg", (i, c // 2), [P, 2, KP], F32, 3)
+            sg = tile_of("sg", (i, c // 2), [P, 2, KP], F32, 4)
             nc.scalar.activation(out=halves(sg[:, c % 2, :]), in_=by_half(flat(live[("z", i, c)])), func=ACT.Sigmoid)
 
         def mul(i, b):
@@ -302,9 +260,9 @@ def tile_regulated_protein_rates_h1_kernel(
                 for u in range(2):
                     nc.tensor.transpose(bank[:, 2 * g + u, :], words[:, P * u:P * (u + 1)], ident[:])
 
-        def c_h(i, b):
-            ht = tile_of("ht", i, [P, GG, KP], BF16, 3)
-            copy_out("scalar", ht[:, 2 * b:2 * b + 2, :], live[("th", i, b)], 2)
+        def c_h(i, b, on_vector=False):
+            ht = tile_of("ht", i, [P, GG, KP], BF16, 2)
+            copy_out(on_vector, ht[:, 2 * b:2 * b + 2, :], live[("th", i, b)], 2)
 
         def q_h(i, k):
             codes = tile_of("hq", i, [P, GG * P], U32, 4)
@@ -338,9 +296,9 @@ def tile_regulated_protein_rates_h1_kernel(
                 in1=by_half(loss[i][:, KP * n:KP * (n + 1)]), op=ALU.subtract,
             )
 
-        def cast(i, k):
+        def cast(i, k, on_vector=False):
             first, stop = ((0, NG), (0, 2), (2, NG))[k]
-            nc.scalar.copy(out=rounded(i, first, stop), in_=by_half(y_sb[i][:, KP * first:KP * stop]))
+            copy(on_vector, rounded(i, first, stop), by_half(y_sb[i][:, KP * first:KP * stop]))
 
         def t_y(i, b):
             bank = new_bank(("ty", i, b))
@@ -350,9 +308,9 @@ def tile_regulated_protein_rates_h1_kernel(
                 for u in range(2):
                     nc.tensor.transpose(bank[:, 2 * g + u, :], words[:, u, first:first + P], ident[:])
 
-        def c_y(i, b):
+        def c_y(i, b, on_vector=False):
             n = min(2, NG - 2 * b)
-            copy_out("scalar", y_turned[:, 2 * b:2 * b + n, KP * i:KP * (i + 1)], live[("ty", i, b)], n)
+            copy_out(on_vector, y_turned[:, 2 * b:2 * b + n, KP * i:KP * (i + 1)], live[("ty", i, b)], n)
 
         def q_y(i, g):
             cols = slice((i - 1) * P, (i + 1) * P)
@@ -383,5 +341,12 @@ def tile_regulated_protein_rates_h1_kernel(
             "t_h": t_h, "c_h": c_h, "q_h": q_h, "mm2": mm2, "dl": dl, "sub": sub, "sub16": sub16,
             "cast": cast, "t_y": t_y, "c_y": c_y, "q_y": q_y, "codes": codes_out, "scales": scales_out,
         }
-        for name, i, k in schedule():
-            steps[name](i, k)
+        todo = pieces()
+        for word in ORDER.split():
+            kind = word.replace("*", "")
+            i, k = todo[kind].pop(0)
+            if word != kind:
+                steps[kind](i, k, True)
+            else:
+                steps[kind](i, k)
+        assert not any(todo.values())

from contextlib import ExitStack

import concourse.mybir as mybir
from concourse.masks import make_identity

S, R, G, N = 768, 1024, 2048, 1536
FLOPS = 2 * S * R * G + 2 * S * G * N

F32 = mybir.dt.float32
BF16 = mybir.dt.bfloat16
I32 = mybir.dt.int32
U32 = mybir.dt.uint32
U8 = mybir.dt.uint8
FP8X4 = mybir.dt.float8_e4m3fn_x4
FP4X4 = mybir.dt.float4_e2m1fn_x4
ACT = mybir.ActivationFunctionType
ALU = mybir.AluOpType

P = 128
KP = 512
TILES = S // P
RG, GG, NG = R // KP, G // KP, N // KP
BANKS = 8


ORDER = """
t_vec t_x c_vec
t_decay c_x* t_decay t_rate q_x mm1 c_rate* c_decay* c_decay t_x t_rate dl
c_x mm1 sig q_x mm1 sig c_rate* mm1 sig t_x mul sig mm1
c_x mm1 mul sig mm1 mm1 sig q_x t_x dl sig t_h c_x t_h mm1 sig mul mm1
sig mm1 q_x c_h mm1 mul c_h mm1 mm1 sig q_h t_x sig mul t_h sig t_h
mm1 sig dl mm2 sig c_x mm2 mul c_h c_h mm1 sub mm2 sig
q_x sig mul mm1 t_h sig sub t_h t_x c_h q_h mm1 c_x mul mm2 c_h
sub mm2 dl cast mm1 mm2 q_x sig sub mm1 sig sub
t_y t_h q_h c_y t_y t_h sub mm1 c_h dl mm1 sig mm2 c_h cast mul mm2
mm1 mul c_y mm1 sig mm2 q_h sig sub sig t_y sub t_h sig
t_h sub mm2 c_h mul c_y mm2 c_h sub cast mm2 mul t_h
q_h t_h c_h t_y sub mm2 c_y sub c_h dl mm2 cast mm2 sub
q_h t_y t_y t_y q_y c_y mm2 sub c_y q_y cast q_y mm2 sub c_y sub
t_y t_y cast mm2 sub c_y q_y c_y cast* t_y codes q_y c_y t_y q_y sub16 c_y scales codes
sub t_y q_y c_y q_y q_y codes codes scales
"""


def pieces():
    tiles = range(TILES)
    table = {}
    for kinds, per_tile in (
        (("t_x", "c_x", "q_x", "q_h", "dl"), 1),
        (("mul", "t_h", "c_h", "t_y", "c_y"), 2),
        (("mm2", "sub"), NG),
        (("mm1", "sig"), GG),
    ):
        for kind in kinds:
            table[kind] = [(i, k) for i in tiles for k in range(per_tile)]
    for kind in ("t_rate", "c_rate", "t_decay", "c_decay"):
        table[kind] = [(0, 0), (0, 1)]
    for kind in ("t_vec", "c_vec"):
        table[kind] = [(0, 0)]
    table["cast"] = [(0, 0), (1, 0), (2, 0), (3, 0), (4, 1), (4, 2), (5, 1)]
    table["sub16"] = [(5, 2)]
    table["q_y"] = [(i, g) for i in (1, 3, 5) for g in range(NG)]
    table["codes"] = [(1, 2), (3, 2), (5, 0), (5, 1)]
    table["scales"] = [(3, 0), (5, 0)]
    return table


def tile_regulated_protein_rates_h1_kernel(
    tc, x, w_words, w_scales, rate, t_words, t_scales, decay, level, out_0, out_1, out_2
):
    nc = tc.nc
    with ExitStack() as ctx:
        keep = ctx.enter_context(tc.tile_pool(name="keep", bufs=1))
        work = ctx.enter_context(tc.tile_pool(name="work", bufs=3))
        psum = ctx.enter_context(tc.psum_pool(name="psum", bufs=1))
        ctx.enter_context(tc.manual_schedule())

        ident = keep.tile([P, P], F32, name="ident")
        w_plane = keep.tile([P, RG, G], U8, name="w_plane", align_bytes=256)
        t_plane = keep.tile([P, GG, N], U8, name="t_plane", align_bytes=256)
        w_sb = keep.tile([P, RG, 2 * G], U8, name="w_sb", align_bytes=256)
        t_sb = keep.tile([P, GG, 2 * N], U8, name="t_sb", align_bytes=256)
        vec = keep.tile([P, KP], BF16, name="vec")
        vec_p = keep.tile([P, 2, 8], F32, name="vec_p")
        rate_all = keep.tile([P, GG, KP], BF16, name="rate_all")
        decay_all = keep.tile([P, NG, KP], BF16, name="decay_all")
        x_sb = [keep.tile([P, R], BF16, name="x%d" % i) for i in range(TILES)]
        level_sb = [keep.tile([P, N], BF16, name="level%d" % i) for i in range(TILES)]
        loss = [keep.tile([P, N], F32, name="loss%d" % i) for i in range(4)]
        loss = [loss[i % 4] for i in range(TILES)]
        y_sb = [keep.tile([P, N], F32, name="y%d" % i) for i in range(4)]
        y_sb = [y_sb[i % 4] for i in range(TILES)]
        y_bf = [keep.tile([P, 2, N // 2], BF16, name="yb%d" % i) for i in range(TILES)]
        y_turned = keep.tile([P, NG, 4 * S], BF16, name="y_turned", align_bytes=256)
        y_codes = keep.tile([P, NG, S], U32, name="y_codes", align_bytes=256)
        y_scales = keep.tile([P, NG, S], U8, name="y_scales", align_bytes=256)
        warm = keep.tile([P, 8], F32, name="warm")
        warm_out = keep.tile([P, 8], F32, name="warm_out")

        nc.gpsimd.memset(vec[:].bitcast(I32), 0)
        nc.vector.memset(w_plane[:, :, :G // 2].bitcast(I32), 0)
        nc.vector.memset(warm[:], 0.0)
        nc.scalar.dma_start(out=vec[0:GG, :], in_=rate.rearrange("(g n) -> g n", g=GG))
        nc.scalar.dma_start(out=vec[GG:GG + NG, :], in_=decay.rearrange("(g n) -> g n", g=NG))
        nc.scalar.activation(out=warm_out[:], in_=warm[:], func=ACT.Sigmoid)
        make_identity(nc, ident[:])
        nc.vector.memset(w_plane[:, :, G // 2:].bitcast(I32), 0)
        nc.vector.memset(t_plane[:].rearrange("p g n -> p (g n)").bitcast(I32), 0)

        def load_rows(dst, src, i):
            nc.sync.dma_start(out=dst[i][:], in_=src[i * P:(i + 1) * P, :])

        def load_scales(plane, scales, cols):
            for q in range(4):
                nc.sync.dma_start(
                    out=plane[32 * q:32 * q + 4, :, cols].bitcast(I32),
                    in_=scales[:, 4 * q:4 * q + 4, cols].rearrange("g r n -> r g n").bitcast(I32),
                )

        def load_words(dst, words, c):
            cols = slice(2 * KP * c, 2 * KP * (c + 1))
            nc.sync.dma_start(
                out=dst[:, :, cols].bitcast(I32),
                in_=words[:, :, cols].rearrange("g p n -> p g n").bitcast(I32),
            )

        load_rows(x_sb, x, 0)
        load_scales(w_plane, w_scales, slice(0, G // 2))
        load_words(w_sb, w_words, 0)
        load_words(w_sb, w_words, 1)
        load_rows(x_sb, x, 1)
        load_rows(level_sb, level, 0)
        load_rows(level_sb, level, 1)
        load_scales(w_plane, w_scales, slice(G // 2, G))
        load_words(w_sb, w_words, 2)
        load_words(w_sb, w_words, 3)
        load_rows(x_sb, x, 2)
        load_scales(t_plane, t_scales, slice(0, N))
        load_rows(x_sb, x, 3)
        load_words(t_sb, t_words, 0)
        load_words(t_sb, t_words, 1)
        load_rows(level_sb, level, 2)
        load_words(t_sb, t_words, 2)
        load_rows(x_sb, x, 4)
        load_rows(level_sb, level, 3)
        load_rows(x_sb, x, 5)
        load_rows(level_sb, level, 4)
        load_rows(level_sb, level, 5)

        live = {}
        used = []

        def new_bank(key):
            tag = "bank%d" % (len(used) % BANKS)
            used.append(key)
            live[key] = psum.tile([P, 4, P], F32, name=tag, tag=tag)
            return live[key]

        def flat(bank):
            return bank[:].rearrange("p a b -> p (a b)")

        def tile_of(kind, i, shape, dtype, bufs):
            if (kind, i) not in live:
                live[(kind, i)] = work.tile(shape, dtype, name=kind, tag=kind, bufs=bufs, align_bytes=256)
            return live[(kind, i)]

        def copy(on_vector, dst, src):
            if on_vector:
                nc.vector.tensor_copy(out=dst, in_=src)
            else:
                nc.scalar.copy(out=dst, in_=src)

        def t_vec(i, k):
            bank = new_bank("vec")
            words = vec[:].bitcast(F32)
            for u in range(2):
                nc.tensor.transpose(bank[:, u, :], words[:, u:256:2], ident[:])

        def c_vec(i, k):
            nc.vector.tensor_copy(out=vec_p[:], in_=live["vec"][:, 0:2, 0:8])

        def spread(kind, row, groups, b):
            bank = new_bank((kind, b))
            for g in range(min(2, groups - 2 * b)):
                r = row + 2 * b + g
                for u in range(2):
                    nc.tensor.transpose(bank[:, 2 * g + u, :], vec_p[:, u, r:r + 1].to_broadcast([P, P]), ident[:])

        def t_rate(i, b):
            spread("rate", 0, GG, b)

        def t_decay(i, b):
            spread("decay", GG, NG, b)

        def c_rate(i, b, on_vector=False):
            dst = rate_all[:, 2 * b:2 * b + 2, :].rearrange("p g n -> p (g n)").bitcast(F32)
            copy(on_vector, dst, flat(live[("rate", b)]))

        def copy_out(on_vector, dst, bank, groups):
            src = bank[:, :2 * groups, :].rearrange("p (g u) s -> p g s u", u=2)
            copy(on_vector, dst.bitcast(F32).rearrange("p g (s u) -> p g s u", u=2), src)

        def c_decay(i, b, on_vector=False):
            n = min(2, NG - 2 * b)
            copy_out(on_vector, decay_all[:, 2 * b:2 * b + n, :], live[("decay", b)], n)

        def t_x(i, k):
            bank = new_bank(("tx", i))
            words = x_sb[i][:].bitcast(F32)
            for g in range(RG):
                for u in range(2):
                    nc.tensor.transpose(bank[:, 2 * g + u, :], words[:, 256 * g + u:256 * (g + 1):2], ident[:])

        def c_x(i, k, on_vector=False):
            xt = tile_of("xt", i, [P, RG, KP], BF16, 2)
            copy_out(on_vector, xt[:], live[("tx", i)], RG)

        def q_x(i, k):
            codes = tile_of("xq", i, [P, RG * P], U32, 3)
            scales = tile_of("xs", i, [P, RG * P], U8, 3)
            nc.vector.quantize_mx(
                out=codes[:].bitcast(FP8X4), scales=scales[:],
                in_=live[("xt", i)][:].rearrange("p g n -> p (g n)"),
            )

        def product(bank, codes, scales, words, plane, groups, c):
            for g in range(groups):
                nc.tensor.matmul_mx(
                    out=flat(bank),
                    lhsT=codes[:, g * P:(g + 1) * P].bitcast(FP8X4),
                    lhsT_scale=scales[:, g * P:(g + 1) * P],
                    rhs=words[:, g, 2 * KP * c:2 * KP * (c + 1)].bitcast(FP4X4),
                    rhs_scale=plane[:, g, KP * c:KP * (c + 1)],
                    start=(g == 0),
                    stop=(g == groups - 1),
                )

        def by_half(ap):
            return ap.rearrange("p (m u e) -> p u m e", u=2, e=2)

        def halves(ap):
            return ap.rearrange("p (u m e) -> p u m e", u=2, e=2)

        def mm1(i, c):
            product(new_bank(("z", i, c)), live[("xq", i)], live[("xs", i)], w_sb, w_plane, RG, c)

        def sig(i, c):
            sg = tile_of("sg", (i, c // 2), [P, 2, KP], F32, 4)
            nc.scalar.activation(out=halves(sg[:, c % 2, :]), in_=by_half(flat(live[("z", i, c)])), func=ACT.Sigmoid)

        def mul(i, b):
            hb = tile_of("hb", i, [P, GG, KP], BF16, 3)
            pair = slice(2 * b, 2 * b + 2)
            nc.vector.tensor_tensor(out=hb[:, pair, :], in0=live[("sg", (i, b))][:], in1=rate_all[:, pair, :], op=ALU.mult)

        def t_h(i, b):
            bank = new_bank(("th", i, b))
            for g in range(2):
                words = live[("hb", i)][:, 2 * b + g, :].bitcast(F32)
                for u in range(2):
                    nc.tensor.transpose(bank[:, 2 * g + u, :], words[:, P * u:P * (u + 1)], ident[:])

        def c_h(i, b, on_vector=False):
            ht = tile_of("ht", i, [P, GG, KP], BF16, 2)
            copy_out(on_vector, ht[:, 2 * b:2 * b + 2, :], live[("th", i, b)], 2)

        def q_h(i, k):
            codes = tile_of("hq", i, [P, GG * P], U32, 4)
            scales = tile_of("hs", i, [P, GG * P], U8, 4)
            nc.vector.quantize_mx(
                out=codes[:].bitcast(FP8X4), scales=scales[:],
                in_=live[("ht", i)][:].rearrange("p g n -> p (g n)"),
            )

        def mm2(i, n):
            product(new_bank(("acc", i, n)), live[("hq", i)], live[("hs", i)], t_sb, t_plane, GG, n)

        def dl(i, k):
            nc.vector.tensor_tensor(
                out=loss[i][:], in0=level_sb[i][:], in1=decay_all[:].rearrange("p g n -> p (g n)"), op=ALU.mult
            )

        def sub(i, n):
            cols = slice(KP * n, KP * (n + 1))
            nc.vector.tensor_tensor(
                out=y_sb[i][:, cols], in0=flat(live[("acc", i, n)]), in1=loss[i][:, cols], op=ALU.subtract
            )
            nc.sync.dma_start(out=out_0[i * P:(i + 1) * P, cols], in_=y_sb[i][:, cols])

        def rounded(i, first, stop):
            return y_bf[i][:].rearrange("p u (m e) -> p u m e", e=2)[:, :, P * first:P * stop, :]

        def sub16(i, n):
            nc.vector.tensor_tensor(
                out=rounded(i, n, n + 1), in0=by_half(flat(live[("acc", i, n)])),
                in1=by_half(loss[i][:, KP * n:KP * (n + 1)]), op=ALU.subtract,
            )

        def cast(i, k, on_vector=False):
            first, stop = ((0, NG), (0, 2), (2, NG))[k]
            copy(on_vector, rounded(i, first, stop), by_half(y_sb[i][:, KP * first:KP * stop]))

        def t_y(i, b):
            bank = new_bank(("ty", i, b))
            words = y_bf[i][:].bitcast(F32)
            for g in range(min(2, NG - 2 * b)):
                first = P * (2 * b + g)
                for u in range(2):
                    nc.tensor.transpose(bank[:, 2 * g + u, :], words[:, u, first:first + P], ident[:])

        def c_y(i, b, on_vector=False):
            n = min(2, NG - 2 * b)
            copy_out(on_vector, y_turned[:, 2 * b:2 * b + n, KP * i:KP * (i + 1)], live[("ty", i, b)], n)

        def q_y(i, g):
            cols = slice((i - 1) * P, (i + 1) * P)
            nc.vector.quantize_mx(
                out=y_codes[:, g, cols].bitcast(FP8X4), scales=y_scales[:, g, cols],
                in_=y_turned[:, g, KP * (i - 1):KP * (i + 1)],
            )

        words_out = out_1.rearrange("g p m t -> p g (m t)").bitcast(I32)

        def codes_out(i, k):
            groups = (slice(0, 2), slice(2, NG), slice(0, NG))[k]
            cols = slice((i - 1) * P, (i + 1) * P)
            nc.sync.dma_start(out=words_out[:, groups, cols], in_=y_codes[:, groups, cols].bitcast(I32))

        def scales_out(i, k):
            cols = slice(0, 4 * P) if i == 3 else slice(4 * P, S)
            for q in range(4):
                eng = nc.scalar if (i == TILES - 1 and q % 2) else nc.sync
                eng.dma_start(
                    out=out_2[:, 4 * q:4 * q + 4, cols].rearrange("g r m -> r g m").bitcast(I32),
                    in_=y_scales[32 * q:32 * q + 4, :, cols].bitcast(I32),
                )

        steps = {
            "t_vec": t_vec, "c_vec": c_vec, "t_rate": t_rate, "t_decay": t_decay, "c_rate": c_rate, "c_decay": c_decay,
            "t_x": t_x, "c_x": c_x, "q_x": q_x, "mm1": mm1, "sig": sig, "mul": mul,
            "t_h": t_h, "c_h": c_h, "q_h": q_h, "mm2": mm2, "dl": dl, "sub": sub, "sub16": sub16,
            "cast": cast, "t_y": t_y, "c_y": c_y, "q_y": q_y, "codes": codes_out, "scales": scales_out,
        }
        todo = pieces()
        for word in ORDER.split():
            kind = word.replace("*", "")
            i, k = todo[kind].pop(0)
            if word != kind:
                steps[kind](i, k, True)
            else:
                steps[kind](i, k)
        assert not any(todo.values())
